import numpy as np
import ml_dtypes


def mxq(x, axis, fmt="e4m3"):
    dtype, down = {"e4m3": (ml_dtypes.float8_e4m3fn, 7), "e5m2": (ml_dtypes.float8_e5m2, 14)}[fmt]
    v = np.moveaxis(np.asarray(x, np.float32).astype(ml_dtypes.bfloat16).astype(np.float64), axis, -1)
    blocks = v.reshape(v.shape[:-1] + (-1, 32))
    amax = np.abs(blocks).max(-1, keepdims=True)
    byte = np.maximum(np.where(amax > 0, np.frexp(amax)[1] - 1 + 127, 0) - down, 1)
    scale = np.exp2(byte - 127.0)
    codes = (blocks / scale).astype(np.float32).astype(dtype).astype(np.float64)
    return np.moveaxis((codes * scale).reshape(v.shape), -1, axis)


WIDE = False


def mx_kscale(k):
    if not WIDE:
        return np.ones(k)
    levels = np.array([10, -10, 5, -5, 0])
    if k % 512:
        return np.exp2(np.random.permutation(np.resize(levels, k // 32))).repeat(32)
    a = np.empty((k // 512, 16))
    for p in range(k // 512):
        a[p, :8] = np.random.permutation(np.resize(levels, 8))
        for g in range(8):
            far = levels[np.abs(levels - a[p, g]) >= 10]
            a[p, g + 8] = far[np.random.randint(len(far))]
    return np.exp2(a.ravel()).repeat(32)


def f64(x):
    return np.asarray(x).astype(np.float64)


def striped(idx):
    return np.tile(np.asarray(idx).reshape(-1, 16).T, (8, 1)).astype(np.uint16)


def unstriped(offs):
    return offs[:16].T.reshape(-1).astype(np.int64)


E2M1 = np.array([0.0, 0.5, 1.0, 1.5, 2.0, 3.0, 4.0, 6.0, -0.0, -0.5, -1.0, -1.5, -2.0, -3.0, -4.0, -6.0])


def pack_weight(w, fmt):
    k, n = w.shape
    w = f64(np.asarray(w, np.float32).astype(ml_dtypes.bfloat16)).reshape(k // 32, 32, n)
    amax = np.abs(w).max(1)
    if fmt == "e4m3":
        byte = np.frexp(amax)[1] - 1 + 127 - 7
    else:
        mant, ex = np.frexp(amax / 6.0)
        byte = np.where(mant > 0.5, ex, ex - 1) + 127
    byte = np.clip(np.where(amax > 0, byte, 1), 1, 254)
    scaled = (w * np.exp2(127.0 - byte)[:, None, :]).reshape(k, n).astype(np.float32)
    by_word = np.ascontiguousarray(scaled.reshape(k // 512, 128, 4, n).transpose(0, 1, 3, 2))
    if fmt == "e4m3":
        words = by_word.astype(ml_dtypes.float8_e4m3fn).view(np.uint8)
    else:
        c = by_word.astype(ml_dtypes.float4_e2m1fn).view(np.uint8) & 0xF
        words = (c[..., 0::2] | (c[..., 1::2] << 4)).reshape(k // 512, 128, 2 * n)
    return np.ascontiguousarray(words), np.ascontiguousarray(byte.astype(np.uint8).reshape(k // 512, 16, n))


def unpack_weight(words, scales, fmt):
    g, _, n = scales.shape
    words = np.ascontiguousarray(words).reshape(g, 128, n, -1)
    if fmt == "e4m3":
        vals = words.view(ml_dtypes.float8_e4m3fn).astype(np.float64)
    else:
        nib = np.empty((g, 128, n, 4), np.uint8)
        nib[..., 0::2] = words & 0xF
        nib[..., 1::2] = words >> 4
        vals = E2M1[nib]
    vals = vals * np.repeat(np.exp2(scales.astype(np.float64) - 127.0), 8, axis=1)[..., None]
    return vals.transpose(0, 1, 3, 2).reshape(g * 512, n)


K, T, J, B, N = 1024, 2048, 512, 64, 512


def setup_inputs():
    n = np.random.standard_normal
    idx = np.random.permutation(T)[:J]
    fk = mx_kscale(K)
    xtp = pack_weight(n((K, T)) / fk[:, None], "e4m3")
    return {
        "xt_words": xtp[0],
        "xt_scales": xtp[1],
        "w": (n((K, N)) * 1 / np.sqrt(K) * fk[:, None]).astype(np.float32),
        "offs": striped(idx),
    }


def reference(xt_words, xt_scales, w, offs):
    idx = unstriped(offs)
    xtu = unpack_weight(xt_words, xt_scales, "e4m3")
    wq = mxq(f64(w), 0, "e4m3")
    xtidxg = xtu[:, idx]
    z = wq.T @ xtidxg
    r1 = z.reshape(N, B, J // B).max(axis=2) + (0.0 - z).reshape(N, B, J // B).max(axis=2)
    m1 = z.reshape(N, B, J // B).mean(axis=2)
    y = r1 / (1.0 + np.abs(m1))
    return y

@@ -1,0 +1,159 @@
+from contextlib import ExitStack
+
+import concourse.mybir as mybir
+
+K, T, J, B, N = 1024, 2048, 512, 64, 512
+FLOPS = 2 * K * N * J
+
+F32 = mybir.dt.float32
+BF16 = mybir.dt.bfloat16
+I32 = mybir.dt.int32
+U32 = mybir.dt.uint32
+U16 = mybir.dt.uint16
+U8 = mybir.dt.uint8
+FP8X4 = mybir.dt.float8_e4m3fn_x4
+ALU = mybir.AluOpType
+ACT = mybir.ActivationFunctionType
+AX = mybir.AxisListType
+
+P = 128
+PACK = 4
+K_PASS = P * PACK
+PASSES = K // K_PASS
+TILES = N // P
+GROUP = J // B
+HALF = J // 2
+
+
+def tile_list_range_of_picked_groups_kernel(tc, xt_words, xt_scales, w, offs, out):
+    nc = tc.nc
+    with ExitStack() as ctx:
+        keep = ctx.enter_context(tc.tile_pool(name="keep", bufs=1))
+        psum = ctx.enter_context(tc.psum_pool(name="psum", bufs=1))
+
+        offsets = keep.tile([P, J // 16], U16, name="offsets")
+        nc.sync.dma_start(offsets[:], offs)
+
+        table_scales = keep.tile([P, T], U8, name="table_scales")
+        nc.gpsimd.memset(table_scales[:].bitcast(I32), 0)
+        for q in range(4):
+            nc.sync.dma_start(
+                table_scales[32 * q : 32 * q + 4 * PASSES, :].bitcast(I32),
+                xt_scales[:, 4 * q : 4 * q + 4, :].bitcast(I32),
+            )
+
+        w_raw = {}
+
+        def load_w(t):
+            for z in range(PASSES):
+                raw = keep.tile([P, PACK, P], F32, name=f"w_raw{t}_{z}")
+                rows = w[z * K_PASS : (z + 1) * K_PASS, t * P : (t + 1) * P]
+                nc.sync.dma_start(raw[:], rows.rearrange("(p r) n -> p r n", r=PACK))
+                w_raw[t, z] = raw
+
+        load_w(0)
+        table = []
+        for z in range(PASSES):
+            words = keep.tile([P, T], I32, name=f"table{z}")
+            nc.sync.dma_start(words[:], xt_words[z].rearrange("p t r -> p (t r)").bitcast(I32))
+            table.append(words)
+        for t in range(1, TILES):
+            load_w(t)
+
+
+        w_codes, w_scales = {}, {}
+
+        def quantise_w(t, z):
+            grouped = keep.tile([P, P, PACK], BF16, name=f"w_bf{t}_{z}", align_bytes=64)
+            nc.scalar.copy(
+                grouped[:].rearrange("p (c i) r -> p c r i", i=4),
+                w_raw[t, z][:].rearrange("p r (c i) -> p c r i", i=4),
+            )
+            codes = keep.tile([P, P], U32, name=f"w_codes{t}_{z}", align_bytes=64)
+            scales = keep.tile([P, P], U8, name=f"w_scales{t}_{z}", align_bytes=64)
+            nc.vector.quantize_mx(
+                out=codes[:].bitcast(FP8X4), scales=scales[:], in_=grouped[:].rearrange("p n r -> p (n r)")
+            )
+            w_codes[t, z], w_scales[t, z] = codes, scales
+
+        x_scales = keep.tile([P, J], U8, name="x_scales", align_bytes=64)
+        x_words = [keep.tile([P, J], U32, name=f"x_words{z}", align_bytes=64) for z in range(PASSES)]
+
+        def gather_words(z, lo, hi):
+            nc.vector.tensor_copy(
+                x_words[z][:, lo:hi], table[z][:].bitcast(U32).indirect(offsets[:, lo // 16 : hi // 16])
+            )
+
+        def spans(t):
+            return [(0, HALF), (HALF, J)] if t in (0, 3) else [(0, J)]
+
+        banks = {}
+
+        def multiply(t, z, lo, hi):
+            if z == 0:
+                banks[t, lo] = psum.tile([P, hi - lo], F32, name=f"z{t}_{lo}")
+            nc.tensor.matmul_mx(
+                out=banks[t, lo][:],
+                lhsT=w_codes[t, z][:].bitcast(FP8X4),
+                lhsT_scale=w_scales[t, z][:],
+                rhs=x_words[z][:, lo:hi].bitcast(FP8X4),
+                rhs_scale=x_scales[4 * z :, lo:hi],
+                start=(z == 0),
+                stop=(z == PASSES - 1),
+            )
+
+        def finish(t):
+            total = keep.tile([P, B], F32, name=f"total{t}")
+            top = keep.tile([P, B], F32, name=f"top{t}")
+            bottom = keep.tile([P, B], F32, name=f"bottom{t}")
+            last = t not in ()
+            for dst, op in ((total, ALU.add), (top, ALU.max), (bottom, ALU.min))[0 if last else 1 :]:
+                for lo, hi in spans(t):
+                    nc.vector.tensor_reduce(
+                        dst[:, lo // GROUP : hi // GROUP],
+                        banks[t, lo][:].rearrange("p (b s) -> p b s", s=GROUP),
+                        AX.X,
+                        op,
+                    )
+            if not last:
+                slots = keep.tile([P, GROUP, B], F32, name=f"slots{t}")
+                for lo, hi in spans(t):
+                    nc.scalar.copy(
+                        slots[:, :, lo // GROUP : hi // GROUP],
+                        banks[t, lo][:].rearrange("p (b s) -> p s b", s=GROUP),
+                    )
+                fours = keep.tile([P, 4, B], F32, name=f"fours{t}")
+                twos = keep.tile([P, 2, B], F32, name=f"twos{t}")
+                nc.gpsimd.tensor_tensor(fours[:], slots[:, 0:4, :], slots[:, 4:8, :], ALU.add)
+                nc.gpsimd.tensor_tensor(twos[:], fours[:, 0:2, :], fours[:, 2:4, :], ALU.add)
+                nc.gpsimd.tensor_tensor(total[:], twos[:, 0, :], twos[:, 1, :], ALU.add)
+            size = keep.tile([P, B], F32, name=f"size{t}")
+            root = keep.tile([P, B], F32, name=f"root{t}")
+            inv = keep.tile([P, B], F32, name=f"inv{t}")
+            nc.scalar.activation(size[:], total[:], ACT.Abs, scale=1.0 / GROUP)
+            nc.scalar.activation(root[:], size[:], ACT.Abs_reciprocal_sqrt, bias=1.0)
+            nc.scalar.activation(inv[:], root[:], ACT.Square)
+            spread = keep.tile([P, B], F32, name=f"spread{t}")
+            y = keep.tile([P, B], F32, name=f"y{t}")
+            eng = nc.gpsimd if t in (0, 1, 2) else nc.vector
+            eng.tensor_tensor(spread[:], top[:], bottom[:], ALU.subtract)
+            eng.tensor_tensor(y[:], spread[:], inv[:], ALU.mult)
+            nc.sync.dma_start(out[t * P : (t + 1) * P, :], y[:])
+
+        for z in range(PASSES):
+            quantise_w(0, z)
+        nc.vector.tensor_copy(x_scales[:], table_scales[:].indirect(offsets[:]))
+        gather_words(0, 0, J)
+        for lo, hi in spans(0):
+            multiply(0, 0, lo, hi)
+        gather_words(1, 0, HALF)
+        gather_words(1, HALF, J)
+        for lo, hi in spans(0):
+            multiply(0, 1, lo, hi)
+        for t in range(1, TILES):
+            for z in range(PASSES):
+                quantise_w(t, z)
+                for lo, hi in spans(t):
+                    multiply(t, z, lo, hi)
+            finish(t - 1)
+        finish(TILES - 1)

@@ -61,6 +61,11 @@ def tile_list_range_of_picked_groups_kernel(tc, xt_words, xt_scales, w, offs, ou
             load_w(t)
 
 
+        warm = keep.tile([P, 8], F32, name="warm")
+        nc.gpsimd.memset(warm[:], 1.0)
+        warm_out = keep.tile([P, 8], F32, name="warm_out")
+        nc.scalar.activation(warm_out[:], warm[:], ACT.Abs_reciprocal_sqrt)
+
         w_codes, w_scales = {}, {}
 
         def quantise_w(t, z):

@@ -1,6 +1,7 @@
 from contextlib import ExitStack
 
 import concourse.mybir as mybir
+from concourse.masks import make_identity
 
 K, T, J, B, N = 1024, 2048, 512, 64, 512
 FLOPS = 2 * K * N * J
@@ -31,17 +32,6 @@ def tile_list_range_of_picked_groups_kernel(tc, xt_words, xt_scales, w, offs, ou
         keep = ctx.enter_context(tc.tile_pool(name="keep", bufs=1))
         psum = ctx.enter_context(tc.psum_pool(name="psum", bufs=1))
 
-        offsets = keep.tile([P, J // 16], U16, name="offsets")
-        nc.sync.dma_start(offsets[:], offs)
-
-        table_scales = keep.tile([P, T], U8, name="table_scales")
-        nc.gpsimd.memset(table_scales[:].bitcast(I32), 0)
-        for q in range(4):
-            nc.sync.dma_start(
-                table_scales[32 * q : 32 * q + 4 * PASSES, :].bitcast(I32),
-                xt_scales[:, 4 * q : 4 * q + 4, :].bitcast(I32),
-            )
-
         w_raw = {}
 
         def load_w(t):
@@ -52,34 +42,50 @@ def tile_list_range_of_picked_groups_kernel(tc, xt_words, xt_scales, w, offs, ou
                 w_raw[t, z] = raw
 
         load_w(0)
-        table = []
-        for z in range(PASSES):
-            words = keep.tile([P, T], I32, name=f"table{z}")
-            nc.sync.dma_start(words[:], xt_words[z].rearrange("p t r -> p (t r)").bitcast(I32))
-            table.append(words)
+        offsets = keep.tile([P, J // 16], U16, name="offsets")
+        nc.sync.dma_start(offsets[:], offs)
+        table_scales = keep.tile([P, T], U8, name="table_scales")
+        nc.gpsimd.memset(table_scales[:].bitcast(I32), 0)
+
+        table = [keep.tile([P, T], I32, name=f"table{z}") for z in range(PASSES)]
+
+        def load_words(z):
+            nc.sync.dma_start(table[z][:], xt_words[z].rearrange("p t r -> p (t r)").bitcast(I32))
+
+        load_words(0)
+        for q in range(4):
+            nc.sync.dma_start(
+                table_scales[32 * q : 32 * q + 4 * PASSES, :].bitcast(I32),
+                xt_scales[:, 4 * q : 4 * q + 4, :].bitcast(I32),
+            )
+        load_words(1)
         for t in range(1, TILES):
             load_w(t)
 
-
         warm = keep.tile([P, 8], F32, name="warm")
-        nc.gpsimd.memset(warm[:], 1.0)
+        nc.vector.memset(warm[:], 1.0)
         warm_out = keep.tile([P, 8], F32, name="warm_out")
         nc.scalar.activation(warm_out[:], warm[:], ACT.Abs_reciprocal_sqrt)
 
+        identity = keep.tile([P, P], F32, name="identity")
+        make_identity(nc, identity[:])
+
         w_codes, w_scales = {}, {}
 
-        def quantise_w(t, z):
-            grouped = keep.tile([P, P, PACK], BF16, name=f"w_bf{t}_{z}", align_bytes=64)
-            nc.scalar.copy(
-                grouped[:].rearrange("p (c i) r -> p c r i", i=4),
-                w_raw[t, z][:].rearrange("p r (c i) -> p c r i", i=4),
-            )
-            codes = keep.tile([P, P], U32, name=f"w_codes{t}_{z}", align_bytes=64)
-            scales = keep.tile([P, P], U8, name=f"w_scales{t}_{z}", align_bytes=64)
+        def quantise_w(t, zs):
+            grouped = keep.tile([P, len(zs), P, PACK], BF16, name=f"w_bf{t}_{zs[0]}", tag=f"w_bf{t}_{zs[0]}", align_bytes=64)
+            for i, z in enumerate(zs):
+                nc.scalar.copy(
+                    grouped[:, i].rearrange("p (c i) r -> p c r i", i=4),
+                    w_raw[t, z][:].rearrange("p r (c i) -> p c r i", i=4),
+                )
+            codes = keep.tile([P, len(zs) * P], U32, name=f"w_codes{t}_{zs[0]}", align_bytes=64)
+            scales = keep.tile([P, len(zs) * P], U8, name=f"w_scales{t}_{zs[0]}", align_bytes=64)
             nc.vector.quantize_mx(
-                out=codes[:].bitcast(FP8X4), scales=scales[:], in_=grouped[:].rearrange("p n r -> p (n r)")
+                out=codes[:].bitcast(FP8X4), scales=scales[:], in_=grouped[:].rearrange("p z n r -> p (z n r)")
             )
-            w_codes[t, z], w_scales[t, z] = codes, scales
+            for i, z in enumerate(zs):
+                w_codes[t, z], w_scales[t, z] = codes[:, i * P : (i + 1) * P], scales[:, i * P : (i + 1) * P]
 
         x_scales = keep.tile([P, J], U8, name="x_scales", align_bytes=64)
         x_words = [keep.tile([P, J], U32, name=f"x_words{z}", align_bytes=64) for z in range(PASSES)]
@@ -90,7 +96,7 @@ def tile_list_range_of_picked_groups_kernel(tc, xt_words, xt_scales, w, offs, ou
             )
 
         def spans(t):
-            return [(0, HALF), (HALF, J)] if t in (0, 3) else [(0, J)]
+            return [(0, HALF), (HALF, J)] if t in (0,) else [(0, J)]
 
         banks = {}
 
@@ -99,54 +105,50 @@ def tile_list_range_of_picked_groups_kernel(tc, xt_words, xt_scales, w, offs, ou
                 banks[t, lo] = psum.tile([P, hi - lo], F32, name=f"z{t}_{lo}")
             nc.tensor.matmul_mx(
                 out=banks[t, lo][:],
-                lhsT=w_codes[t, z][:].bitcast(FP8X4),
-                lhsT_scale=w_scales[t, z][:],
+                lhsT=w_codes[t, z].bitcast(FP8X4),
+                lhsT_scale=w_scales[t, z],
                 rhs=x_words[z][:, lo:hi].bitcast(FP8X4),
                 rhs_scale=x_scales[4 * z :, lo:hi],
                 start=(z == 0),
                 stop=(z == PASSES - 1),
             )
 
-        def finish(t):
+        def product(t, groups):
+            for zs in groups:
+                quantise_w(t, zs)
+                for z in zs:
+                    for lo, hi in spans(t):
+                        multiply(t, z, lo, hi)
+
+        def reduce_groups(dst, t, lo, hi, op):
+            nc.vector.tensor_reduce(
+                dst[:, lo // GROUP : hi // GROUP], banks[t, lo][:].rearrange("p (b s) -> p b s", s=GROUP), AX.X, op
+            )
+
+        def inverse(total, width, name):
+            size = keep.tile([P, width], F32, name=f"size{name}")
+            root = keep.tile([P, width], F32, name=f"root{name}")
+            inv = keep.tile([P, width], F32, name=f"inv{name}")
+            nc.scalar.activation(size[:], total, ACT.Abs, scale=1.0 / GROUP)
+            nc.scalar.activation(root[:], size[:], ACT.Abs_reciprocal_sqrt, bias=1.0)
+            nc.scalar.activation(inv[:], root[:], ACT.Square)
+            return inv
+
+        def finish(t, eng):
             total = keep.tile([P, B], F32, name=f"total{t}")
             top = keep.tile([P, B], F32, name=f"top{t}")
             bottom = keep.tile([P, B], F32, name=f"bottom{t}")
-            last = t not in ()
-            for dst, op in ((total, ALU.add), (top, ALU.max), (bottom, ALU.min))[0 if last else 1 :]:
+            for dst, op in ((total, ALU.add), (top, ALU.max), (bottom, ALU.min)):
                 for lo, hi in spans(t):
-                    nc.vector.tensor_reduce(
-                        dst[:, lo // GROUP : hi // GROUP],
-                        banks[t, lo][:].rearrange("p (b s) -> p b s", s=GROUP),
-                        AX.X,
-                        op,
-                    )
-            if not last:
-                slots = keep.tile([P, GROUP, B], F32, name=f"slots{t}")
-                for lo, hi in spans(t):
-                    nc.scalar.copy(
-                        slots[:, :, lo // GROUP : hi // GROUP],
-                        banks[t, lo][:].rearrange("p (b s) -> p s b", s=GROUP),
-                    )
-                fours = keep.tile([P, 4, B], F32, name=f"fours{t}")
-                twos = keep.tile([P, 2, B], F32, name=f"twos{t}")
-                nc.gpsimd.tensor_tensor(fours[:], slots[:, 0:4, :], slots[:, 4:8, :], ALU.add)
-                nc.gpsimd.tensor_tensor(twos[:], fours[:, 0:2, :], fours[:, 2:4, :], ALU.add)
-                nc.gpsimd.tensor_tensor(total[:], twos[:, 0, :], twos[:, 1, :], ALU.add)
-            size = keep.tile([P, B], F32, name=f"size{t}")
-            root = keep.tile([P, B], F32, name=f"root{t}")
-            inv = keep.tile([P, B], F32, name=f"inv{t}")
-            nc.scalar.activation(size[:], total[:], ACT.Abs, scale=1.0 / GROUP)
-            nc.scalar.activation(root[:], size[:], ACT.Abs_reciprocal_sqrt, bias=1.0)
-            nc.scalar.activation(inv[:], root[:], ACT.Square)
+                    reduce_groups(dst, t, lo, hi, op)
+            inv = inverse(total[:], B, t)
             spread = keep.tile([P, B], F32, name=f"spread{t}")
             y = keep.tile([P, B], F32, name=f"y{t}")
-            eng = nc.gpsimd if t in (0, 1, 2) else nc.vector
             eng.tensor_tensor(spread[:], top[:], bottom[:], ALU.subtract)
             eng.tensor_tensor(y[:], spread[:], inv[:], ALU.mult)
             nc.sync.dma_start(out[t * P : (t + 1) * P, :], y[:])
 
-        for z in range(PASSES):
-            quantise_w(0, z)
+        quantise_w(0, (0, 1))
         nc.vector.tensor_copy(x_scales[:], table_scales[:].indirect(offsets[:]))
         gather_words(0, 0, J)
         for lo, hi in spans(0):
@@ -155,10 +157,46 @@ def tile_list_range_of_picked_groups_kernel(tc, xt_words, xt_scales, w, offs, ou
         gather_words(1, HALF, J)
         for lo, hi in spans(0):
             multiply(0, 1, lo, hi)
-        for t in range(1, TILES):
-            for z in range(PASSES):
-                quantise_w(t, z)
-                for lo, hi in spans(t):
-                    multiply(t, z, lo, hi)
-            finish(t - 1)
-        finish(TILES - 1)
+
+        def extremes(t, top, bottom):
+            for lo, hi in spans(t):
+                reduce_groups(bottom, t, lo, hi, ALU.min)
+                reduce_groups(top, t, lo, hi, ALU.max)
+
+        product(1, [(0,), (1,)])
+        tops = [keep.tile([P, B], F32, name="top0")]
+        bottoms = [keep.tile([P, B], F32, name="bottom0")]
+        extremes(0, tops[0], bottoms[0])
+        product(2, [(0,), (1,)])
+        tops.append(keep.tile([P, B], F32, name="top1", tag="w_bf2_1", align_bytes=64))
+        bottoms.append(keep.tile([P, B], F32, name="bottom1", tag="w_bf2_0", align_bytes=64))
+        extremes(1, tops[1], bottoms[1])
+        product(3, [(0,), (1,)])
+
+        slots = keep.tile([P, GROUP, 2 * B], F32, name="slots")
+        spread2 = keep.tile([P, 2 * B], F32, name="spread_pair")
+        for t in range(2):
+            for lo, hi in spans(t):
+                nc.scalar.copy(
+                    slots[:, :, t * B + lo // GROUP : t * B + hi // GROUP],
+                    banks[t, lo][:].rearrange("p (b s) -> p s b", s=GROUP),
+                )
+            nc.gpsimd.tensor_tensor(spread2[:, t * B : (t + 1) * B], tops[t][:], bottoms[t][:], ALU.subtract)
+        total_t = psum.tile([P, P], F32, name="total_t")
+        for s in range(GROUP):
+            nc.tensor.matmul(
+                total_t[:], slots[:, s, :], identity[:], start=(s == 0), stop=(s == GROUP - 1), is_transpose=True
+            )
+        size_t = keep.tile([P, P], F32, name="size_t")
+        nc.scalar.activation(size_t[:], total_t[:], ACT.Abs, scale=1.0 / GROUP)
+        size2 = psum.tile([P, P], F32, name="size_pair")
+        nc.tensor.transpose(size2[:], size_t[:], identity[:])
+        root2 = keep.tile([P, P], F32, name="root_pair")
+        inv2 = keep.tile([P, P], F32, name="inv_pair")
+        nc.scalar.activation(root2[:], size2[:], ACT.Abs_reciprocal_sqrt, bias=1.0)
+        nc.scalar.activation(inv2[:], root2[:], ACT.Square)
+        y2 = keep.tile([P, 2, B], F32, name="y_pair")
+        nc.gpsimd.tensor_tensor(y2[:].rearrange("p t b -> p (t b)"), spread2[:], inv2[:], ALU.mult)
+        nc.sync.dma_start(out[0 : 2 * P, :].rearrange("(t p) b -> p t b", p=P), y2[:])
+        finish(2, nc.gpsimd)
+        finish(3, nc.vector)

@@ -41,29 +41,29 @@ def tile_list_range_of_picked_groups_kernel(tc, xt_words, xt_scales, w, offs, ou
                 nc.sync.dma_start(raw[:], rows.rearrange("(p r) n -> p r n", r=PACK))
                 w_raw[t, z] = raw
 
-        load_w(0)
         offsets = keep.tile([P, J // 16], U16, name="offsets")
         nc.sync.dma_start(offsets[:], offs)
-        table_scales = keep.tile([P, T], U8, name="table_scales")
-        nc.gpsimd.memset(table_scales[:].bitcast(I32), 0)
-
         table = [keep.tile([P, T], I32, name=f"table{z}") for z in range(PASSES)]
 
         def load_words(z):
             nc.sync.dma_start(table[z][:], xt_words[z].rearrange("p t r -> p (t r)").bitcast(I32))
 
         load_words(0)
+        table_scales = keep.tile([P, T], U8, name="table_scales")
+        nc.vector.memset(table_scales[:].bitcast(I32), 0)
         for q in range(4):
             nc.sync.dma_start(
                 table_scales[32 * q : 32 * q + 4 * PASSES, :].bitcast(I32),
                 xt_scales[:, 4 * q : 4 * q + 4, :].bitcast(I32),
             )
+
+        load_w(0)
         load_words(1)
         for t in range(1, TILES):
             load_w(t)
 
         warm = keep.tile([P, 8], F32, name="warm")
-        nc.vector.memset(warm[:], 1.0)
+        nc.gpsimd.memset(warm[:], 1.0)
         warm_out = keep.tile([P, 8], F32, name="warm_out")
         nc.scalar.activation(warm_out[:], warm[:], ACT.Abs_reciprocal_sqrt)
 
@@ -96,7 +96,7 @@ def tile_list_range_of_picked_groups_kernel(tc, xt_words, xt_scales, w, offs, ou
             )
 
         def spans(t):
-            return [(0, HALF), (HALF, J)] if t in (0,) else [(0, J)]
+            return [(0, HALF), (HALF, J)] if t in (0, 1) else [(0, J)]
 
         banks = {}
 
@@ -148,9 +148,10 @@ def tile_list_range_of_picked_groups_kernel(tc, xt_words, xt_scales, w, offs, ou
             eng.tensor_tensor(y[:], spread[:], inv[:], ALU.mult)
             nc.sync.dma_start(out[t * P : (t + 1) * P, :], y[:])
 
-        quantise_w(0, (0, 1))
-        nc.vector.tensor_copy(x_scales[:], table_scales[:].indirect(offsets[:]))
         gather_words(0, 0, J)
+        nc.vector.tensor_copy(x_scales[:], table_scales[:].indirect(offsets[:]))
+        quantise_w(0, (0,))
+        quantise_w(0, (1,))
         for lo, hi in spans(0):
             multiply(0, 0, lo, hi)
         gather_words(1, 0, HALF)

@@ -48,16 +48,21 @@ def tile_list_range_of_picked_groups_kernel(tc, xt_words, xt_scales, w, offs, ou
         def load_words(z):
             nc.sync.dma_start(table[z][:], xt_words[z].rearrange("p t r -> p (t r)").bitcast(I32))
 
-        load_words(0)
         table_scales = keep.tile([P, T], U8, name="table_scales")
         nc.vector.memset(table_scales[:].bitcast(I32), 0)
-        for q in range(4):
-            nc.sync.dma_start(
-                table_scales[32 * q : 32 * q + 4 * PASSES, :].bitcast(I32),
-                xt_scales[:, 4 * q : 4 * q + 4, :].bitcast(I32),
-            )
+
+        def load_scales(q):
+            for z in range(PASSES):
+                nc.sync.dma_start(
+                    table_scales[32 * q + 4 * z : 32 * q + 4 * z + 4, :].bitcast(I32),
+                    xt_scales[z, 4 * q : 4 * q + 4, :].bitcast(I32),
+                )
 
         load_w(0)
+        load_scales(0)
+        load_words(0)
+        for q in range(1, 4):
+            load_scales(q)
         load_words(1)
         for t in range(1, TILES):
             load_w(t)
@@ -96,13 +101,13 @@ def tile_list_range_of_picked_groups_kernel(tc, xt_words, xt_scales, w, offs, ou
             )
 
         def spans(t):
-            return [(0, HALF), (HALF, J)] if t in (0, 1) else [(0, J)]
+            return [(0, HALF), (HALF, J)] if t in (0, 1, 3) else [(0, J)]
 
         banks = {}
 
         def multiply(t, z, lo, hi):
             if z == 0:
-                banks[t, lo] = psum.tile([P, hi - lo], F32, name=f"z{t}_{lo}")
+                banks[t, lo] = psum.tile([P, hi - lo], F32, name=f"z{t}_{lo}", tag=f"z{t}_{lo}")
             nc.tensor.matmul_mx(
                 out=banks[t, lo][:],
                 lhsT=w_codes[t, z].bitcast(FP8X4),
@@ -148,10 +153,10 @@ def tile_list_range_of_picked_groups_kernel(tc, xt_words, xt_scales, w, offs, ou
             eng.tensor_tensor(y[:], spread[:], inv[:], ALU.mult)
             nc.sync.dma_start(out[t * P : (t + 1) * P, :], y[:])
 
-        gather_words(0, 0, J)
-        nc.vector.tensor_copy(x_scales[:], table_scales[:].indirect(offsets[:]))
         quantise_w(0, (0,))
         quantise_w(0, (1,))
+        gather_words(0, 0, J)
+        nc.vector.tensor_copy(x_scales[:], table_scales[:].indirect(offsets[:]))
         for lo, hi in spans(0):
             multiply(0, 0, lo, hi)
         gather_words(1, 0, HALF)
@@ -164,24 +169,28 @@ def tile_list_range_of_picked_groups_kernel(tc, xt_words, xt_scales, w, offs, ou
                 reduce_groups(bottom, t, lo, hi, ALU.min)
                 reduce_groups(top, t, lo, hi, ALU.max)
 
-        product(1, [(0,), (1,)])
-        tops = [keep.tile([P, B], F32, name="top0")]
-        bottoms = [keep.tile([P, B], F32, name="bottom0")]
-        extremes(0, tops[0], bottoms[0])
-        product(2, [(0,), (1,)])
-        tops.append(keep.tile([P, B], F32, name="top1", tag="w_bf2_1", align_bytes=64))
-        bottoms.append(keep.tile([P, B], F32, name="bottom1", tag="w_bf2_0", align_bytes=64))
-        extremes(1, tops[1], bottoms[1])
-        product(3, [(0,), (1,)])
-
         slots = keep.tile([P, GROUP, 2 * B], F32, name="slots")
-        spread2 = keep.tile([P, 2 * B], F32, name="spread_pair")
-        for t in range(2):
+
+        def copy_slots(t):
             for lo, hi in spans(t):
                 nc.scalar.copy(
                     slots[:, :, t * B + lo // GROUP : t * B + hi // GROUP],
                     banks[t, lo][:].rearrange("p (b s) -> p s b", s=GROUP),
                 )
+
+        product(1, [(0,), (1,)])
+        tops = [keep.tile([P, B], F32, name="top0")]
+        bottoms = [keep.tile([P, B], F32, name="bottom0")]
+        extremes(0, tops[0], bottoms[0])
+        product(2, [(0,), (1,)])
+        copy_slots(0)
+        tops.append(keep.tile([P, B], F32, name="top1", tag="w_bf2_1", align_bytes=64))
+        bottoms.append(keep.tile([P, B], F32, name="bottom1", tag="w_bf2_0", align_bytes=64))
+        extremes(1, tops[1], bottoms[1])
+        product(3, [(0,), (1,)])
+        copy_slots(1)
+        spread2 = keep.tile([P, 2 * B], F32, name="spread_pair", tag="w_bf3_1", align_bytes=64)
+        for t in range(2):
             nc.gpsimd.tensor_tensor(spread2[:, t * B : (t + 1) * B], tops[t][:], bottoms[t][:], ALU.subtract)
         total_t = psum.tile([P, P], F32, name="total_t")
         for s in range(GROUP):
@@ -190,7 +199,7 @@ def tile_list_range_of_picked_groups_kernel(tc, xt_words, xt_scales, w, offs, ou
             )
         size_t = keep.tile([P, P], F32, name="size_t")
         nc.scalar.activation(size_t[:], total_t[:], ACT.Abs, scale=1.0 / GROUP)
-        size2 = psum.tile([P, P], F32, name="size_pair")
+        size2 = psum.tile([P, P], F32, name="size_pair", tag="z0_0")
         nc.tensor.transpose(size2[:], size_t[:], identity[:])
         root2 = keep.tile([P, P], F32, name="root_pair")
         inv2 = keep.tile([P, P], F32, name="inv_pair")

from contextlib import ExitStack

import concourse.mybir as mybir
from concourse.masks import make_identity

K, T, J, B, N = 1024, 2048, 512, 64, 512
FLOPS = 2 * K * N * J

F32 = mybir.dt.float32
BF16 = mybir.dt.bfloat16
I32 = mybir.dt.int32
U32 = mybir.dt.uint32
U16 = mybir.dt.uint16
U8 = mybir.dt.uint8
FP8X4 = mybir.dt.float8_e4m3fn_x4
ALU = mybir.AluOpType
ACT = mybir.ActivationFunctionType
AX = mybir.AxisListType

P = 128
PACK = 4
K_PASS = P * PACK
PASSES = K // K_PASS
TILES = N // P
GROUP = J // B
HALF = J // 2


def tile_list_range_of_picked_groups_kernel(tc, xt_words, xt_scales, w, offs, out):
    nc = tc.nc
    with ExitStack() as ctx:
        keep = ctx.enter_context(tc.tile_pool(name="keep", bufs=1))
        psum = ctx.enter_context(tc.psum_pool(name="psum", bufs=1))

        w_raw = {}

        def load_w(t):
            for z in range(PASSES):
                raw = keep.tile([P, PACK, P], F32, name=f"w_raw{t}_{z}")
                rows = w[z * K_PASS : (z + 1) * K_PASS, t * P : (t + 1) * P]
                nc.sync.dma_start(raw[:], rows.rearrange("(p r) n -> p r n", r=PACK))
                w_raw[t, z] = raw

        offsets = keep.tile([P, J // 16], U16, name="offsets")
        nc.sync.dma_start(offsets[:], offs)
        table = [keep.tile([P, T], I32, name=f"table{z}") for z in range(PASSES)]

        def load_words(z):
            nc.sync.dma_start(table[z][:], xt_words[z].rearrange("p t r -> p (t r)").bitcast(I32))

        table_scales = keep.tile([P, T], U8, name="table_scales")
        nc.vector.memset(table_scales[:].bitcast(I32), 0)

        def load_scales(q):
            for z in range(PASSES):
                nc.sync.dma_start(
                    table_scales[32 * q + 4 * z : 32 * q + 4 * z + 4, :].bitcast(I32),
                    xt_scales[z, 4 * q : 4 * q + 4, :].bitcast(I32),
                )

        load_w(0)
        load_scales(0)
        load_words(0)
        for q in range(1, 4):
            load_scales(q)
        load_words(1)
        for t in range(1, TILES):
            load_w(t)

        warm = keep.tile([P, 8], F32, name="warm")
        nc.gpsimd.memset(warm[:], 1.0)
        warm_out = keep.tile([P, 8], F32, name="warm_out")
        nc.scalar.activation(warm_out[:], warm[:], ACT.Abs_reciprocal_sqrt)

        identity = keep.tile([P, P], F32, name="identity")
        make_identity(nc, identity[:])

        w_codes, w_scales = {}, {}

        def quantise_w(t, zs):
            grouped = keep.tile([P, len(zs), P, PACK], BF16, name=f"w_bf{t}_{zs[0]}", tag=f"w_bf{t}_{zs[0]}", align_bytes=64)
            for i, z in enumerate(zs):
                nc.scalar.copy(
                    grouped[:, i].rearrange("p (c i) r -> p c r i", i=4),
                    w_raw[t, z][:].rearrange("p r (c i) -> p c r i", i=4),
                )
            codes = keep.tile([P, len(zs) * P], U32, name=f"w_codes{t}_{zs[0]}", align_bytes=64)
            scales = keep.tile([P, len(zs) * P], U8, name=f"w_scales{t}_{zs[0]}", align_bytes=64)
            nc.vector.quantize_mx(
                out=codes[:].bitcast(FP8X4), scales=scales[:], in_=grouped[:].rearrange("p z n r -> p (z n r)")
            )
            for i, z in enumerate(zs):
                w_codes[t, z], w_scales[t, z] = codes[:, i * P : (i + 1) * P], scales[:, i * P : (i + 1) * P]

        x_scales = keep.tile([P, J], U8, name="x_scales", align_bytes=64)
        x_words = [keep.tile([P, J], U32, name=f"x_words{z}", align_bytes=64) for z in range(PASSES)]

        def gather_words(z, lo, hi):
            nc.vector.tensor_copy(
                x_words[z][:, lo:hi], table[z][:].bitcast(U32).indirect(offsets[:, lo // 16 : hi // 16])
            )

        def spans(t):
            return [(0, HALF), (HALF, J)] if t in (0, 1, 3) else [(0, J)]

        banks = {}

        def multiply(t, z, lo, hi):
            if z == 0:
                banks[t, lo] = psum.tile([P, hi - lo], F32, name=f"z{t}_{lo}", tag=f"z{t}_{lo}")
            nc.tensor.matmul_mx(
                out=banks[t, lo][:],
                lhsT=w_codes[t, z].bitcast(FP8X4),
                lhsT_scale=w_scales[t, z],
                rhs=x_words[z][:, lo:hi].bitcast(FP8X4),
                rhs_scale=x_scales[4 * z :, lo:hi],
                start=(z == 0),
                stop=(z == PASSES - 1),
            )

        def product(t, groups):
            for zs in groups:
                quantise_w(t, zs)
                for z in zs:
                    for lo, hi in spans(t):
                        multiply(t, z, lo, hi)

        def reduce_groups(dst, t, lo, hi, op):
            nc.vector.tensor_reduce(
                dst[:, lo // GROUP : hi // GROUP], banks[t, lo][:].rearrange("p (b s) -> p b s", s=GROUP), AX.X, op
            )

        def inverse(total, width, name):
            size = keep.tile([P, width], F32, name=f"size{name}")
            root = keep.tile([P, width], F32, name=f"root{name}")
            inv = keep.tile([P, width], F32, name=f"inv{name}")
            nc.scalar.activation(size[:], total, ACT.Abs, scale=1.0 / GROUP)
            nc.scalar.activation(root[:], size[:], ACT.Abs_reciprocal_sqrt, bias=1.0)
            nc.scalar.activation(inv[:], root[:], ACT.Square)
            return inv

        def finish(t, eng):
            total = keep.tile([P, B], F32, name=f"total{t}")
            top = keep.tile([P, B], F32, name=f"top{t}")
            bottom = keep.tile([P, B], F32, name=f"bottom{t}")
            for dst, op in ((total, ALU.add), (top, ALU.max), (bottom, ALU.min)):
                for lo, hi in spans(t):
                    reduce_groups(dst, t, lo, hi, op)
            inv = inverse(total[:], B, t)
            spread = keep.tile([P, B], F32, name=f"spread{t}")
            y = keep.tile([P, B], F32, name=f"y{t}")
            eng.tensor_tensor(spread[:], top[:], bottom[:], ALU.subtract)
            eng.tensor_tensor(y[:], spread[:], inv[:], ALU.mult)
            nc.sync.dma_start(out[t * P : (t + 1) * P, :], y[:])

        quantise_w(0, (0,))
        quantise_w(0, (1,))
        gather_words(0, 0, J)
        nc.vector.tensor_copy(x_scales[:], table_scales[:].indirect(offsets[:]))
        for lo, hi in spans(0):
            multiply(0, 0, lo, hi)
        gather_words(1, 0, HALF)
        gather_words(1, HALF, J)
        for lo, hi in spans(0):
            multiply(0, 1, lo, hi)

        def extremes(t, top, bottom):
            for lo, hi in spans(t):
                reduce_groups(bottom, t, lo, hi, ALU.min)
                reduce_groups(top, t, lo, hi, ALU.max)

        slots = keep.tile([P, GROUP, 2 * B], F32, name="slots")

        def copy_slots(t):
            for lo, hi in spans(t):
                nc.scalar.copy(
                    slots[:, :, t * B + lo // GROUP : t * B + hi // GROUP],
                    banks[t, lo][:].rearrange("p (b s) -> p s b", s=GROUP),
                )

        product(1, [(0,), (1,)])
        tops = [keep.tile([P, B], F32, name="top0")]
        bottoms = [keep.tile([P, B], F32, name="bottom0")]
        extremes(0, tops[0], bottoms[0])
        product(2, [(0,), (1,)])
        copy_slots(0)
        tops.append(keep.tile([P, B], F32, name="top1", tag="w_bf2_1", align_bytes=64))
        bottoms.append(keep.tile([P, B], F32, name="bottom1", tag="w_bf2_0", align_bytes=64))
        extremes(1, tops[1], bottoms[1])
        product(3, [(0,), (1,)])
        copy_slots(1)
        spread2 = keep.tile([P, 2 * B], F32, name="spread_pair", tag="w_bf3_1", align_bytes=64)
        for t in range(2):
            nc.gpsimd.tensor_tensor(spread2[:, t * B : (t + 1) * B], tops[t][:], bottoms[t][:], ALU.subtract)
        total_t = psum.tile([P, P], F32, name="total_t")
        for s in range(GROUP):
            nc.tensor.matmul(
                total_t[:], slots[:, s, :], identity[:], start=(s == 0), stop=(s == GROUP - 1), is_transpose=True
            )
        size_t = keep.tile([P, P], F32, name="size_t")
        nc.scalar.activation(size_t[:], total_t[:], ACT.Abs, scale=1.0 / GROUP)
        size2 = psum.tile([P, P], F32, name="size_pair", tag="z0_0")
        nc.tensor.transpose(size2[:], size_t[:], identity[:])
        root2 = keep.tile([P, P], F32, name="root_pair")
        inv2 = keep.tile([P, P], F32, name="inv_pair")
        nc.scalar.activation(root2[:], size2[:], ACT.Abs_reciprocal_sqrt, bias=1.0)
        nc.scalar.activation(inv2[:], root2[:], ACT.Square)
        y2 = keep.tile([P, 2, B], F32, name="y_pair")
        nc.gpsimd.tensor_tensor(y2[:].rearrange("p t b -> p (t b)"), spread2[:], inv2[:], ALU.mult)
        nc.sync.dma_start(out[0 : 2 * P, :].rearrange("(t p) b -> p t b", p=P), y2[:])
        finish(2, nc.gpsimd)
        finish(3, nc.vector)
